import numpy as np
import ml_dtypes


def mxq(x, axis, fmt="e4m3"):
    dtype, down = {"e4m3": (ml_dtypes.float8_e4m3fn, 7), "e5m2": (ml_dtypes.float8_e5m2, 14)}[fmt]
    v = np.moveaxis(np.asarray(x, np.float32).astype(ml_dtypes.bfloat16).astype(np.float64), axis, -1)
    blocks = v.reshape(v.shape[:-1] + (-1, 32))
    amax = np.abs(blocks).max(-1, keepdims=True)
    byte = np.maximum(np.where(amax > 0, np.frexp(amax)[1] - 1 + 127, 0) - down, 1)
    scale = np.exp2(byte - 127.0)
    codes = (blocks / scale).astype(np.float32).astype(dtype).astype(np.float64)
    return np.moveaxis((codes * scale).reshape(v.shape), -1, axis)


WIDE = False


def mx_kscale(k):
    if not WIDE:
        return np.ones(k)
    levels = np.array([10, -10, 5, -5, 0])
    if k % 512:
        return np.exp2(np.random.permutation(np.resize(levels, k // 32))).repeat(32)
    a = np.empty((k // 512, 16))
    for p in range(k // 512):
        a[p, :8] = np.random.permutation(np.resize(levels, 8))
        for g in range(8):
            far = levels[np.abs(levels - a[p, g]) >= 10]
            a[p, g + 8] = far[np.random.randint(len(far))]
    return np.exp2(a.ravel()).repeat(32)


def f64(x):
    return np.asarray(x).astype(np.float64)


def striped(idx):
    return np.tile(idx.reshape(-1, 16).T, (8, 1)).astype(np.uint16)


def unstriped(offs):
    return offs[:16].T.reshape(-1).astype(np.int64)


E2M1 = np.array([0.0, 0.5, 1.0, 1.5, 2.0, 3.0, 4.0, 6.0, -0.0, -0.5, -1.0, -1.5, -2.0, -3.0, -4.0, -6.0])


def pack_weight(w, fmt):
    k, n = w.shape
    w = f64(np.asarray(w, np.float32).astype(ml_dtypes.bfloat16)).reshape(k // 32, 32, n)
    amax = np.abs(w).max(1)
    if fmt == "e4m3":
        byte = np.frexp(amax)[1] - 1 + 127 - 7
    else:
        mant, ex = np.frexp(amax / 6.0)
        byte = np.where(mant > 0.5, ex, ex - 1) + 127
    byte = np.clip(np.where(amax > 0, byte, 1), 1, 254)
    scaled = (w * np.exp2(127.0 - byte)[:, None, :]).reshape(k, n).astype(np.float32)
    by_word = np.ascontiguousarray(scaled.reshape(k // 512, 128, 4, n).transpose(0, 1, 3, 2))
    if fmt == "e4m3":
        words = by_word.astype(ml_dtypes.float8_e4m3fn).view(np.uint8)
    else:
        c = by_word.astype(ml_dtypes.float4_e2m1fn).view(np.uint8) & 0xF
        words = (c[..., 0::2] | (c[..., 1::2] << 4)).reshape(k // 512, 128, 2 * n)
    return np.ascontiguousarray(words), np.ascontiguousarray(byte.astype(np.uint8).reshape(k // 512, 16, n))


def unpack_weight(words, scales, fmt):
    g, _, n = scales.shape
    words = np.ascontiguousarray(words).reshape(g, 128, n, -1)
    if fmt == "e4m3":
        vals = words.view(ml_dtypes.float8_e4m3fn).astype(np.float64)
    else:
        nib = np.empty((g, 128, n, 4), np.uint8)
        nib[..., 0::2] = words & 0xF
        nib[..., 1::2] = words >> 4
        vals = E2M1[nib]
    vals = vals * np.repeat(np.exp2(scales.astype(np.float64) - 127.0), 8, axis=1)[..., None]
    return vals.transpose(0, 1, 3, 2).reshape(g * 512, n)


def gelu(v):
    return 0.5 * v * (1.0 + np.tanh(np.sqrt(2.0 / np.pi) * (v + 0.044715 * v**3)))


K, H, T, S, T2, P = 1536, 512, 4096, 1024, 2048, 1024

def setup_inputs():
    n = np.random.standard_normal
    s = mx_kscale(K)[:, None]
    u = mx_kscale(H)[:, None]
    d = {}
    d["tab_words"], d["tab_scales"] = pack_weight(n((K, T)) * s, "e4m3")
    d["offs"] = striped(np.random.permutation(T)[:S])
    d["w1"] = (n((K, H)) / s / K ** 0.5).astype(np.float32)
    d["w2_words"], d["w2_scales"] = pack_weight(n((K, H)) / s / K ** 0.5, "e2m1")
    d["gain"] = (np.exp(0.3 * n(H)) * u[:, 0]).astype(np.float32)
    d["page0"] = (n((H, T2)) * u).astype(np.float32)
    d["offs2"] = striped(np.random.permutation(T2)[:S])
    d["wgs"] = np.exp(0.3 * n((128, S))).astype(np.float32)
    d["offs3"] = striped(np.random.permutation(T2)[:P])
    d["offs4"] = striped(np.random.permutation(T2)[:P])
    d["sc"] = np.exp(0.3 * n(H)).astype(np.float32)
    d["w3_words"], d["w3_scales"] = pack_weight(n((H, H)) / u / H ** 0.5, "e2m1")
    d["w4"] = (n((H, H)) / u / H ** 0.5).astype(np.float32)
    d["gv"] = (np.exp(0.3 * n(H)) / u[:, 0]).astype(np.float32)
    return d

def reference(tab_words, tab_scales, offs, w1, w2_words, w2_scales, gain, page0, offs2, wgs, offs3, offs4, sc, w3_words, w3_scales, w4, gv):
    v = unpack_weight(tab_words, tab_scales, "e4m3")[:, unstriped(offs)]
    a = mxq(f64(w1), 0, "e4m3").T @ v
    b = unpack_weight(w2_words, w2_scales, "e2m1").T @ v
    h = f64(gain)[:, None] * np.tanh(a + np.abs(b))
    page = f64(page0).copy()
    page[:, unstriped(offs2)] = np.tile(f64(wgs), (H // 128, 1)) * h
    x = page[:, unstriped(offs3)] * f64(sc)[:, None]
    y3 = unpack_weight(w3_words, w3_scales, "e2m1").T @ mxq(x, 0, "e4m3")
    y4 = mxq(f64(w4), 0, "e4m3").T @ mxq(np.abs(x), 0, "e4m3")
    nxt = page[:, unstriped(offs4)] * f64(gv)[:, None]
    return np.minimum(y3, y4) * nxt

@@ -1,0 +1,315 @@
+from contextlib import ExitStack
+
+import concourse.mybir as mybir
+from concourse.masks import make_identity
+
+K, H, T, S, T2, M = 1536, 512, 4096, 1024, 2048, 1024
+FLOPS = 2 * (2 * K * H * S + 2 * H * H * M)
+
+F32 = mybir.dt.float32
+BF16 = mybir.dt.bfloat16
+I32 = mybir.dt.int32
+U32 = mybir.dt.uint32
+U16 = mybir.dt.uint16
+U8 = mybir.dt.uint8
+FP8X4 = mybir.dt.float8_e4m3fn_x4
+FP4X4 = mybir.dt.float4_e2m1fn_x4
+ACT = mybir.ActivationFunctionType
+ALU = mybir.AluOpType
+
+P = 128
+PACK = 4
+K_PASS = P * PACK
+PASSES = K // K_PASS
+BLOCKS = H // P
+HALF = 512
+HALVES = S // HALF
+GROUPS = HALF // P
+LIST_COLS = HALF // 16
+LIVE_ROWS = 100
+SPARE_ROWS = 32 - 4 * PASSES
+VEC_ROW = P - 3 * BLOCKS
+
+
+def tile_list_tufting_needle_page_kernel(
+    tc, tab_words, tab_scales, offs, w1, w2_words, w2_scales, gain, page0, offs2, wgs, offs3, offs4, sc,
+    w3_words, w3_scales, w4, gv, out,
+):
+    nc = tc.nc
+    with ExitStack() as ctx:
+        keep = ctx.enter_context(tc.tile_pool(name="keep", bufs=1))
+        ring = ctx.enter_context(tc.tile_pool(name="ring", bufs=2))
+        psum = ctx.enter_context(tc.psum_pool(name="psum", bufs=2))
+
+        def cols(i, width):
+            return slice(i * width, (i + 1) * width)
+
+        def load_list(name, src):
+            lst = keep.tile([P, S // 16], U16, name=name)
+            nc.sync.dma_start(lst[:], src)
+            return lst
+
+        def half_list(lst, h):
+            return lst[:, cols(h, LIST_COLS)]
+
+        def zeroed_bytes(name, shape):
+            t = keep.tile(shape, U8, name=name, align_bytes=64)
+            nc.gpsimd.memset(t[:].bitcast(I32), 0)
+            return t
+
+        scale_window = keep.tile([P, T], U8, name="scale_window")
+        for q in range(4):
+            nc.vector.memset(scale_window[32 * q : 32 * q + SPARE_ROWS, :].bitcast(I32), 0)
+            nc.scalar.dma_start(
+                out=scale_window[32 * q + SPARE_ROWS : 32 * (q + 1), :].bitcast(I32),
+                in_=tab_scales[:, 4 * q : 4 * q + 4, :].bitcast(I32),
+            )
+        idx = load_list("idx", offs)
+        w2_plane = zeroed_bytes("w2_plane", [P, PASSES, H])
+        moved = [zeroed_bytes("moved%d" % a, [P, S]) for a in range(PASSES)]
+        picked_scales = keep.tile([P, S], U8, name="picked_scales", align_bytes=64)
+        nc.vector.tensor_copy(out=picked_scales[:], in_=scale_window[:].indirect(idx[:]))
+        for a in range(PASSES):
+            first_row = SPARE_ROWS + 4 * a
+            nc.gpsimd.dma_start(
+                out=moved[a][:LIVE_ROWS, :].bitcast(I32),
+                in_=picked_scales[first_row : first_row + LIVE_ROWS, :].bitcast(I32),
+            )
+        for q in range(4):
+            nc.gpsimd.dma_start(
+                out=w2_plane[32 * q : 32 * q + 4].bitcast(I32),
+                in_=w2_scales[:, 4 * q : 4 * q + 4, :].rearrange("a r c -> r a c").bitcast(I32),
+            )
+        vec_rows = keep.tile([P, P], F32, name="vec_rows")
+        nc.vector.memset(vec_rows[:VEC_ROW, :], 0.0)
+        warm = keep.tile([P, 1], F32, name="warm")
+        nc.vector.memset(warm[:], 0.0)
+        nc.scalar.activation(out=warm[:], in_=warm[:], func=ACT.Tanh)
+        w3_plane = zeroed_bytes("w3_plane", [P, H])
+        ident = keep.tile([P, P], F32, name="ident")
+        make_identity(nc, ident[:])
+        ident_bf = keep.tile([P, P], BF16, name="ident_bf")
+        make_identity(nc, ident_bf[:])
+
+        tab = [keep.tile([P, T], U32, name="tab%d" % a) for a in range(PASSES)]
+
+        def load_tab(a):
+            nc.sync.dma_start(out=tab[a][:].bitcast(I32), in_=tab_words[a].rearrange("p t i -> p (t i)").bitcast(I32))
+
+        w1_raw = {}
+
+        def load_w1(b):
+            for a in range(PASSES):
+                raw = ring.tile([P, PACK, P], F32, name="w1_raw", bufs=6)
+                nc.sync.dma_start(out=raw[:], in_=w1[cols(a, K_PASS), cols(b, P)].rearrange("(p j) c -> p j c", j=PACK))
+                w1_raw[b, a] = raw
+
+        page = [keep.tile([P, T2], F32, name="page%d" % b) for b in range(BLOCKS)]
+
+        def load_page(b):
+            nc.sync.dma_start(out=page[b][:], in_=page0[cols(b, P), :])
+
+        load_tab(0)
+        load_w1(0)
+        w2_codes = keep.tile([P, PASSES, 2 * H], U8, name="w2_codes", align_bytes=64)
+        nc.sync.dma_start(out=w2_codes[:].bitcast(I32), in_=w2_words.rearrange("a p c -> p a c").bitcast(I32))
+        load_tab(1)
+        load_tab(2)
+        for i, src in enumerate((gain, sc, gv)):
+            nc.sync.dma_start(
+                out=vec_rows[VEC_ROW + i * BLOCKS : VEC_ROW + (i + 1) * BLOCKS, :],
+                in_=src.rearrange("(b c) -> b c", c=P),
+            )
+        wgs_sb = keep.tile([P, S], F32, name="wgs_sb")
+        nc.sync.dma_start(out=wgs_sb[:], in_=wgs)
+        idx2 = load_list("idx2", offs2)
+        load_page(0)
+        load_w1(1)
+        idx3 = load_list("idx3", offs3)
+
+        vec_ps = psum.tile([P, P], F32, name="vec_ps", tag="bank_d")
+        nc.tensor.transpose(vec_ps[:], vec_rows[:], ident[:])
+        vec = keep.tile([P, 3 * BLOCKS], F32, name="vec")
+        nc.scalar.copy(out=vec[:], in_=vec_ps[:, VEC_ROW:])
+
+        def row_factor(i, b):
+            return vec[:, i * BLOCKS + b : i * BLOCKS + b + 1]
+
+        picked = {}
+        for a in range(PASSES):
+            for h in range(HALVES):
+                words = keep.tile([P, HALF], U32, name="picked%d_%d" % (a, h), align_bytes=64)
+                nc.vector.tensor_copy(out=words[:], in_=tab[a][:].indirect(half_list(idx, h)))
+                picked[a, h] = words
+
+        def quantise(name, grouped, width):
+            codes = keep.tile([P, width], U32, name=name + "_codes", align_bytes=64)
+            plane = keep.tile([P, width], U8, name=name + "_plane", align_bytes=64)
+            nc.vector.quantize_mx(out=codes[:].bitcast(FP8X4), scales=plane[:], in_=grouped)
+            return codes, plane
+
+        def quantise_weight(name, raw, grouped, width):
+            nc.scalar.copy(out=grouped.rearrange("p (c j) -> p c j", j=PACK), in_=raw[:].rearrange("p j c -> p c j"))
+            return quantise(name, grouped, width)
+
+        w1_q = {}
+
+        def prepare_w1(b):
+            grouped = ring.tile([P, PASSES * K_PASS], BF16, name="w1_grouped", align_bytes=64, bufs=4)
+            for a in range(PASSES):
+                w1_q[b, a] = quantise_weight("w1_%d_%d" % (b, a), w1_raw[b, a], grouped[:, cols(a, K_PASS)], P)
+            return grouped
+
+        prepare_w1(0)
+        gw = {}
+
+        def weigh(b, h, dst):
+            nc.vector.tensor_scalar(dst, wgs_sb[:, cols(h, HALF)], row_factor(0, b), None, ALU.mult)
+            gw[b, h] = dst
+
+        for b in range(BLOCKS):
+            for h in range(HALVES):
+                if (b, h) != (0, 1):
+                    t = keep.tile([P, HALF], F32, name="gw%d_%d" % (b, h))
+                    weigh(b, h, t[:])
+
+        spent = {}
+
+        def first_stage(b, h):
+            acc_a = psum.tile([P, HALF], F32, name="acc_a", tag="bank_a")
+            acc_b = psum.tile([P, HALF], F32, name="acc_b", tag="bank_b")
+            for a in range(PASSES):
+                codes, plane = w1_q[b, a]
+                moving = (
+                    (acc_a, codes[:].bitcast(FP8X4), plane[:]),
+                    (acc_b, w2_codes[:, a, cols(b, 2 * P)].bitcast(FP4X4), w2_plane[:, a, cols(b, P)]),
+                )
+                for acc, weight, weight_plane in moving:
+                    for g in range(GROUPS):
+                        nc.tensor.matmul_mx(
+                            out=acc[:, cols(g, P)],
+                            lhsT=picked[a, h][:, cols(g, P)].bitcast(FP8X4),
+                            lhsT_scale=moved[a][:, cols(h * GROUPS + g, P)],
+                            rhs=weight,
+                            rhs_scale=weight_plane,
+                            start=a == 0 and g == 0,
+                            stop=a == PASSES - 1 and g == GROUPS - 1,
+                        )
+            sum_a = ring.tile([P, HALF], F32, name="sum_a", tag="left", bufs=4)
+            spent[b, h] = sum_a
+            nc.scalar.copy(out=sum_a[:], in_=acc_a[:])
+            abs_b = ring.tile([P, HALF], F32, name="abs_b", tag="right", bufs=4)
+            nc.scalar.activation(out=abs_b[:], in_=acc_b[:], func=ACT.Abs)
+            pre = psum.tile([P, HALF], F32, name="pre", tag="bank_c")
+            for term, src in enumerate((sum_a, abs_b)):
+                for g in range(GROUPS):
+                    nc.tensor.matmul(
+                        pre[:, cols(g, P)], lhsT=src[:, cols(g, P)], rhs=ident[:], is_transpose=True,
+                        start=term == 0 and g == 0, stop=term == 1 and g == GROUPS - 1,
+                    )
+            act = ring.tile([P, HALF], F32, name="act", tag="piece", bufs=4)
+            nc.scalar.activation(out=act[:], in_=pre[:], func=ACT.Tanh)
+            nc.vector.tensor_tensor(page[b][:].indirect(half_list(idx2, h)), act[:], gw[b, h], ALU.mult)
+
+        nxt = {}
+
+        def gather_next(b):
+            for h in range(HALVES):
+                t = gw[b ^ (b >> 1), h]
+                nc.vector.tensor_copy(out=t, in_=page[b][:].indirect(half_list(idx4, h)))
+                nxt[b, h] = t
+
+        turned = [keep.tile([P, GROUPS, 2, P], F32, name="turned%d" % h) for h in range(HALVES)]
+
+        def reread(b):
+            if b + 1 < BLOCKS:
+                holder = spent[b + 1, HALVES - 1]
+            else:
+                holder = ring.tile([P, HALF], F32, name="holder", tag="left", bufs=4)
+            for h in range(HALVES):
+                got = ring.tile([P, HALF], F32, name="got", bufs=2)
+                nc.vector.tensor_copy(out=got[:], in_=page[b][:].indirect(half_list(idx3, h)))
+                x_rows = holder[:].bitcast(BF16)[:, cols(h, HALF)]
+                nc.scalar.activation(out=x_rows, in_=got[:], func=ACT.Copy, scale=row_factor(1, b))
+                x_ps = psum.tile([P, HALF], BF16, name="x_ps", tag="bank_d")
+                for g in range(GROUPS):
+                    nc.tensor.transpose(x_ps[:, cols(g, P)], x_rows[:, cols(g, P)], ident_bf[:])
+                nc.scalar.copy(
+                    out=turned[h][:, :, :, cols(b, 32)],
+                    in_=x_ps[:].bitcast(F32).rearrange("p (g q u) -> p g u q", g=GROUPS, u=2),
+                )
+
+        for b in range(BLOCKS):
+            if b + 2 < BLOCKS:
+                load_w1(b + 2)
+            if b + 1 < BLOCKS:
+                load_page(b + 1)
+            first_stage(b, 0)
+            if b == 0:
+                weigh(0, 1, prepare_w1(1)[:, K_PASS:].bitcast(F32))
+            first_stage(b, 1)
+            if b + 2 < BLOCKS:
+                prepare_w1(b + 2)
+            if b > 0:
+                reread(b - 1)
+
+        w4_raw = keep.tile([P, PACK, H], F32, name="w4_raw")
+        nc.sync.dma_start(out=w4_raw[:], in_=w4.rearrange("(p j) c -> p j c", j=PACK))
+        w3_codes = keep.tile([P, 2 * H], U8, name="w3_codes", align_bytes=64)
+        nc.sync.dma_start(out=w3_codes[:].bitcast(I32), in_=w3_words[0].bitcast(I32))
+        for q in range(4):
+            nc.sync.dma_start(
+                out=w3_plane[32 * q : 32 * q + 4, :].bitcast(I32),
+                in_=w3_scales[0, 4 * q : 4 * q + 4, :].bitcast(I32),
+            )
+        idx4 = load_list("idx4", offs4)
+        w4_grouped = ring.tile([P, H * PACK], BF16, name="w4_grouped", tag="abs_x", align_bytes=64)
+        w4_codes, w4_plane = quantise_weight("w4", w4_raw, w4_grouped[:], H)
+
+        def turn_back(h):
+            x_words = ring.tile([P, HALF, 2], F32, name="x_words", align_bytes=64)
+            for pair in range(GROUPS // 2):
+                back = psum.tile([P, 2, 2, P], F32, name="back", tag="bank_c")
+                for g in range(2):
+                    for u in range(2):
+                        nc.tensor.transpose(back[:, g, u, :], turned[h][:, 2 * pair + g, u, :], ident[:])
+                nc.scalar.copy(
+                    out=x_words[:, cols(pair, 2 * P), :].rearrange("p (g m) u -> p g m u", g=2),
+                    in_=back[:].rearrange("p g u m -> p g m u"),
+                )
+            return x_words[:].rearrange("p m u -> p (m u)").bitcast(BF16)
+
+        def quantise_x(h, x_grouped):
+            abs_x = ring.tile([P, HALF, PACK], BF16, name="abs_x", tag="abs_x", align_bytes=64)
+            abs_grouped = abs_x[:].rearrange("p m j -> p (m j)")
+            for pair in range(2):
+                part = cols(pair, PACK * HALF // 2)
+                nc.scalar.activation(out=abs_grouped[:, part], in_=x_grouped[:, part], func=ACT.Abs)
+            return quantise("x%d" % h, x_grouped, HALF), quantise("abs_x%d" % h, abs_grouped, HALF)
+
+        def second_stage(h, x_q, abs_q):
+            for b in range(BLOCKS):
+                y3 = psum.tile([P, HALF], F32, name="y3", tag="bank_a")
+                y4 = psum.tile([P, HALF], F32, name="y4", tag="bank_b")
+                nc.tensor.matmul_mx(
+                    out=y3[:], lhsT=w3_codes[:, cols(b, 2 * P)].bitcast(FP4X4), lhsT_scale=w3_plane[:, cols(b, P)],
+                    rhs=x_q[0][:].bitcast(FP8X4), rhs_scale=x_q[1][:], start=True, stop=True,
+                )
+                nc.tensor.matmul_mx(
+                    out=y4[:], lhsT=w4_codes[:, cols(b, P)].bitcast(FP8X4), lhsT_scale=w4_plane[:, cols(b, P)],
+                    rhs=abs_q[0][:].bitcast(FP8X4), rhs_scale=abs_q[1][:], start=True, stop=True,
+                )
+                y3_sb = ring.tile([P, HALF], F32, name="y3_sb", tag="left", bufs=4)
+                nc.scalar.copy(out=y3_sb[:], in_=y3[:])
+                low = ring.tile([P, HALF], F32, name="low", tag="right", bufs=4)
+                nc.vector.tensor_tensor(low[:], y4[:], y3_sb[:], ALU.min)
+                nc.vector.scalar_tensor_tensor(low[:], low[:], row_factor(2, b), nxt[b, h], ALU.mult, ALU.mult)
+                nc.sync.dma_start(out=out[cols(b, P), cols(h, HALF)], in_=low[:])
+
+        reread(BLOCKS - 1)
+        for b in range(BLOCKS):
+            gather_next(b)
+        first_q = quantise_x(0, turn_back(0))
+        x_later = turn_back(1)
+        second_stage(0, *first_q)
+        second_stage(1, *quantise_x(1, x_later))

@@ -52,12 +52,17 @@ def tile_list_tufting_needle_page_kernel(
         def half_list(lst, h):
             return lst[:, cols(h, LIST_COLS)]
 
-        def zeroed_bytes(name, shape):
+        def zeroed_bytes(engine, name, shape):
             t = keep.tile(shape, U8, name=name, align_bytes=64)
-            nc.gpsimd.memset(t[:].bitcast(I32), 0)
+            engine.memset(t[:].bitcast(I32), 0)
             return t
 
-        scale_window = keep.tile([P, T], U8, name="scale_window")
+        ident = keep.tile([P, P], F32, name="ident")
+        make_identity(nc, ident[:])
+        ident_bf = keep.tile([P, P], BF16, name="ident_bf")
+        make_identity(nc, ident_bf[:])
+        w2_plane = zeroed_bytes(nc.vector, "w2_plane", [P, PASSES, H])
+        scale_window = keep.tile([P, T], U8, name="scale_window", tag="last_window")
         for q in range(4):
             nc.vector.memset(scale_window[32 * q : 32 * q + SPARE_ROWS, :].bitcast(I32), 0)
             nc.scalar.dma_start(
@@ -65,41 +70,31 @@ def tile_list_tufting_needle_page_kernel(
                 in_=tab_scales[:, 4 * q : 4 * q + 4, :].bitcast(I32),
             )
         idx = load_list("idx", offs)
-        w2_plane = zeroed_bytes("w2_plane", [P, PASSES, H])
-        moved = [zeroed_bytes("moved%d" % a, [P, S]) for a in range(PASSES)]
+        moved = [zeroed_bytes(nc.gpsimd, "moved%d" % a, [P, S]) for a in range(PASSES)]
         picked_scales = keep.tile([P, S], U8, name="picked_scales", align_bytes=64)
         nc.vector.tensor_copy(out=picked_scales[:], in_=scale_window[:].indirect(idx[:]))
-        for a in range(PASSES):
-            first_row = SPARE_ROWS + 4 * a
-            nc.gpsimd.dma_start(
-                out=moved[a][:LIVE_ROWS, :].bitcast(I32),
-                in_=picked_scales[first_row : first_row + LIVE_ROWS, :].bitcast(I32),
-            )
-        for q in range(4):
-            nc.gpsimd.dma_start(
-                out=w2_plane[32 * q : 32 * q + 4].bitcast(I32),
-                in_=w2_scales[:, 4 * q : 4 * q + 4, :].rearrange("a r c -> r a c").bitcast(I32),
-            )
         vec_rows = keep.tile([P, P], F32, name="vec_rows")
-        nc.vector.memset(vec_rows[:VEC_ROW, :], 0.0)
+        nc.gpsimd.memset(vec_rows[:VEC_ROW, :], 0.0)
+        for i, src in enumerate((gain, sc, gv)):
+            nc.gpsimd.dma_start(
+                out=vec_rows[VEC_ROW + i * BLOCKS : VEC_ROW + (i + 1) * BLOCKS, :],
+                in_=src.rearrange("(b c) -> b c", c=P),
+            )
         warm = keep.tile([P, 1], F32, name="warm")
         nc.vector.memset(warm[:], 0.0)
         nc.scalar.activation(out=warm[:], in_=warm[:], func=ACT.Tanh)
-        w3_plane = zeroed_bytes("w3_plane", [P, H])
-        ident = keep.tile([P, P], F32, name="ident")
-        make_identity(nc, ident[:])
-        ident_bf = keep.tile([P, P], BF16, name="ident_bf")
-        make_identity(nc, ident_bf[:])
+        w3_plane = zeroed_bytes(nc.vector, "w3_plane", [P, H])
 
-        tab = [keep.tile([P, T], U32, name="tab%d" % a) for a in range(PASSES)]
+        tab = [keep.tile([P, T], U32, name="tab%d" % a) for a in range(PASSES - 1)]
+        tab.append(keep.tile([P, T], U32, name="tab_last", tag="last_window"))
 
         def load_tab(a):
             nc.sync.dma_start(out=tab[a][:].bitcast(I32), in_=tab_words[a].rearrange("p t i -> p (t i)").bitcast(I32))
 
         w1_raw = {}
 
-        def load_w1(b):
-            for a in range(PASSES):
+        def load_w1(b, passes=range(PASSES)):
+            for a in passes:
                 raw = ring.tile([P, PACK, P], F32, name="w1_raw", bufs=6)
                 nc.sync.dma_start(out=raw[:], in_=w1[cols(a, K_PASS), cols(b, P)].rearrange("(p j) c -> p j c", j=PACK))
                 w1_raw[b, a] = raw
@@ -110,16 +105,23 @@ def tile_list_tufting_needle_page_kernel(
             nc.sync.dma_start(out=page[b][:], in_=page0[cols(b, P), :])
 
         load_tab(0)
-        load_w1(0)
+        load_w1(0, range(PASSES - 1))
+        for q in range(4):
+            nc.sync.dma_start(
+                out=w2_plane[32 * q : 32 * q + 4].bitcast(I32),
+                in_=w2_scales[:, 4 * q : 4 * q + 4, :].rearrange("a r c -> r a c").bitcast(I32),
+            )
+        load_tab(1)
+        load_w1(0, [PASSES - 1])
         w2_codes = keep.tile([P, PASSES, 2 * H], U8, name="w2_codes", align_bytes=64)
         nc.sync.dma_start(out=w2_codes[:].bitcast(I32), in_=w2_words.rearrange("a p c -> p a c").bitcast(I32))
-        load_tab(1)
-        load_tab(2)
-        for i, src in enumerate((gain, sc, gv)):
+        for a in range(PASSES):
+            first_row = SPARE_ROWS + 4 * a
             nc.sync.dma_start(
-                out=vec_rows[VEC_ROW + i * BLOCKS : VEC_ROW + (i + 1) * BLOCKS, :],
-                in_=src.rearrange("(b c) -> b c", c=P),
+                out=moved[a][:LIVE_ROWS, :].bitcast(I32),
+                in_=picked_scales[first_row : first_row + LIVE_ROWS, :].bitcast(I32),
             )
+        load_tab(2)
         wgs_sb = keep.tile([P, S], F32, name="wgs_sb")
         nc.sync.dma_start(out=wgs_sb[:], in_=wgs)
         idx2 = load_list("idx2", offs2)
@@ -163,19 +165,20 @@ def tile_list_tufting_needle_page_kernel(
         prepare_w1(0)
         gw = {}
 
-        def weigh(b, h, dst):
-            nc.vector.tensor_scalar(dst, wgs_sb[:, cols(h, HALF)], row_factor(0, b), None, ALU.mult)
-            gw[b, h] = dst
+        def weigh(dst, b, entries):
+            nc.vector.tensor_scalar(dst, wgs_sb[:, entries], row_factor(0, b), None, ALU.mult)
+            return dst
 
-        for b in range(BLOCKS):
-            for h in range(HALVES):
-                if (b, h) != (0, 1):
-                    t = keep.tile([P, HALF], F32, name="gw%d_%d" % (b, h))
-                    weigh(b, h, t[:])
+        gw_first = keep.tile([P, HALF], F32, name="gw_first")
+        gw[0, 0] = weigh(gw_first[:], 0, cols(0, HALF))
+        for b in range(1, BLOCKS):
+            t = keep.tile([P, S], F32, name="gw%d" % b)
+            gw[b] = weigh(t[:], b, cols(0, S))
+        gw[1, 0], gw[1, 1] = gw[1][:, cols(0, HALF)], gw[1][:, cols(1, HALF)]
 
         spent = {}
 
-        def first_stage(b, h):
+        def first_stage(b, h, act):
             acc_a = psum.tile([P, HALF], F32, name="acc_a", tag="bank_a")
             acc_b = psum.tile([P, HALF], F32, name="acc_b", tag="bank_b")
             for a in range(PASSES):
@@ -207,17 +210,23 @@ def tile_list_tufting_needle_page_kernel(
                         pre[:, cols(g, P)], lhsT=src[:, cols(g, P)], rhs=ident[:], is_transpose=True,
                         start=term == 0 and g == 0, stop=term == 1 and g == GROUPS - 1,
                     )
-            act = ring.tile([P, HALF], F32, name="act", tag="piece", bufs=4)
-            nc.scalar.activation(out=act[:], in_=pre[:], func=ACT.Tanh)
-            nc.vector.tensor_tensor(page[b][:].indirect(half_list(idx2, h)), act[:], gw[b, h], ALU.mult)
+            nc.scalar.activation(out=act[:, cols(h, HALF)], in_=pre[:], func=ACT.Tanh)
+
+        def scatter(b, offsets, values, weights):
+            nc.vector.tensor_tensor(page[b][:].indirect(offsets), values, weights, ALU.mult)
 
         nxt = {}
 
         def gather_next(b):
-            for h in range(HALVES):
-                t = gw[b ^ (b >> 1), h]
-                nc.vector.tensor_copy(out=t, in_=page[b][:].indirect(half_list(idx4, h)))
-                nxt[b, h] = t
+            if b == 0:
+                for h in range(HALVES):
+                    nc.vector.tensor_copy(out=gw[0, h], in_=page[b][:].indirect(half_list(idx4, h)))
+                    nxt[b, h] = gw[0, h]
+            else:
+                dst = gw[b ^ (b >> 1)]
+                nc.vector.tensor_copy(out=dst, in_=page[b][:].indirect(idx4[:]))
+                for h in range(HALVES):
+                    nxt[b, h] = dst[:, cols(h, HALF)]
 
         turned = [keep.tile([P, GROUPS, 2, P], F32, name="turned%d" % h) for h in range(HALVES)]
 
@@ -226,11 +235,15 @@ def tile_list_tufting_needle_page_kernel(
                 holder = spent[b + 1, HALVES - 1]
             else:
                 holder = ring.tile([P, HALF], F32, name="holder", tag="left", bufs=4)
+            got = ring.tile([P, M], F32, name="got")
+            if b + 1 < BLOCKS:
+                nc.vector.tensor_copy(out=got[:], in_=page[b][:].indirect(idx3[:]))
+            else:
+                for h in range(HALVES):
+                    nc.vector.tensor_copy(out=got[:, cols(h, HALF)], in_=page[b][:].indirect(half_list(idx3, h)))
             for h in range(HALVES):
-                got = ring.tile([P, HALF], F32, name="got", bufs=2)
-                nc.vector.tensor_copy(out=got[:], in_=page[b][:].indirect(half_list(idx3, h)))
                 x_rows = holder[:].bitcast(BF16)[:, cols(h, HALF)]
-                nc.scalar.activation(out=x_rows, in_=got[:], func=ACT.Copy, scale=row_factor(1, b))
+                nc.scalar.activation(out=x_rows, in_=got[:, cols(h, HALF)], func=ACT.Copy, scale=row_factor(1, b))
                 x_ps = psum.tile([P, HALF], BF16, name="x_ps", tag="bank_d")
                 for g in range(GROUPS):
                     nc.tensor.transpose(x_ps[:, cols(g, P)], x_rows[:, cols(g, P)], ident_bf[:])
@@ -244,10 +257,17 @@ def tile_list_tufting_needle_page_kernel(
                 load_w1(b + 2)
             if b + 1 < BLOCKS:
                 load_page(b + 1)
-            first_stage(b, 0)
+            act = ring.tile([P, S], F32, name="act")
+            first_stage(b, 0, act)
+            if b < 2:
+                scatter(b, half_list(idx2, 0), act[:, cols(0, HALF)], gw[b, 0])
             if b == 0:
-                weigh(0, 1, prepare_w1(1)[:, K_PASS:].bitcast(F32))
-            first_stage(b, 1)
+                gw[0, 1] = weigh(prepare_w1(1)[:, K_PASS:].bitcast(F32), 0, cols(1, HALF))
+            first_stage(b, 1, act)
+            if b < 2:
+                scatter(b, half_list(idx2, 1), act[:, cols(1, HALF)], gw[b, 1])
+            else:
+                scatter(b, idx2[:], act[:], gw[b])
             if b + 2 < BLOCKS:
                 prepare_w1(b + 2)
             if b > 0:
@@ -287,6 +307,13 @@ def tile_list_tufting_needle_page_kernel(
                 nc.scalar.activation(out=abs_grouped[:, part], in_=x_grouped[:, part], func=ACT.Abs)
             return quantise("x%d" % h, x_grouped, HALF), quantise("abs_x%d" % h, abs_grouped, HALF)
 
+        lows = {}
+
+        def finish(b, h):
+            low = lows[b, h]
+            nc.vector.scalar_tensor_tensor(low[:], low[:], row_factor(2, b), nxt[b, h], ALU.mult, ALU.mult)
+            nc.sync.dma_start(out=out[cols(b, P), cols(h, HALF)], in_=low[:])
+
         def second_stage(h, x_q, abs_q):
             for b in range(BLOCKS):
                 y3 = psum.tile([P, HALF], F32, name="y3", tag="bank_a")
@@ -303,8 +330,10 @@ def tile_list_tufting_needle_page_kernel(
                 nc.scalar.copy(out=y3_sb[:], in_=y3[:])
                 low = ring.tile([P, HALF], F32, name="low", tag="right", bufs=4)
                 nc.vector.tensor_tensor(low[:], y4[:], y3_sb[:], ALU.min)
-                nc.vector.scalar_tensor_tensor(low[:], low[:], row_factor(2, b), nxt[b, h], ALU.mult, ALU.mult)
-                nc.sync.dma_start(out=out[cols(b, P), cols(h, HALF)], in_=low[:])
+                lows[b, h] = low
+                if b > 0:
+                    finish(b - 1, h)
+            finish(BLOCKS - 1, h)
 
         reread(BLOCKS - 1)
         for b in range(BLOCKS):

@@ -38,6 +38,7 @@ def tile_list_tufting_needle_page_kernel(
     nc = tc.nc
     with ExitStack() as ctx:
         keep = ctx.enter_context(tc.tile_pool(name="keep", bufs=1))
+        shared = ctx.enter_context(tc.tile_pool(name="shared", bufs=1))
         ring = ctx.enter_context(tc.tile_pool(name="ring", bufs=2))
         psum = ctx.enter_context(tc.psum_pool(name="psum", bufs=2))
 
@@ -62,7 +63,7 @@ def tile_list_tufting_needle_page_kernel(
         ident_bf = keep.tile([P, P], BF16, name="ident_bf")
         make_identity(nc, ident_bf[:])
         w2_plane = zeroed_bytes(nc.vector, "w2_plane", [P, PASSES, H])
-        scale_window = keep.tile([P, T], U8, name="scale_window", tag="last_window")
+        scale_window = shared.tile([P, T], U8, name="scale_window", offset=2 * S)
         for q in range(4):
             nc.vector.memset(scale_window[32 * q : 32 * q + SPARE_ROWS, :].bitcast(I32), 0)
             nc.scalar.dma_start(
@@ -73,6 +74,11 @@ def tile_list_tufting_needle_page_kernel(
         moved = [zeroed_bytes(nc.gpsimd, "moved%d" % a, [P, S]) for a in range(PASSES)]
         picked_scales = keep.tile([P, S], U8, name="picked_scales", align_bytes=64)
         nc.vector.tensor_copy(out=picked_scales[:], in_=scale_window[:].indirect(idx[:]))
+        for q in range(4):
+            nc.gpsimd.dma_start(
+                out=w2_plane[32 * q : 32 * q + 4].bitcast(I32),
+                in_=w2_scales[:, 4 * q : 4 * q + 4, :].rearrange("a r c -> r a c").bitcast(I32),
+            )
         vec_rows = keep.tile([P, P], F32, name="vec_rows")
         nc.gpsimd.memset(vec_rows[:VEC_ROW, :], 0.0)
         for i, src in enumerate((gain, sc, gv)):
@@ -86,16 +92,16 @@ def tile_list_tufting_needle_page_kernel(
         w3_plane = zeroed_bytes(nc.vector, "w3_plane", [P, H])
 
         tab = [keep.tile([P, T], U32, name="tab%d" % a) for a in range(PASSES - 1)]
-        tab.append(keep.tile([P, T], U32, name="tab_last", tag="last_window"))
+        tab.append(shared.tile([P, T], U32, name="tab_last", offset=4 * S))
 
         def load_tab(a):
             nc.sync.dma_start(out=tab[a][:].bitcast(I32), in_=tab_words[a].rearrange("p t i -> p (t i)").bitcast(I32))
 
         w1_raw = {}
 
-        def load_w1(b, passes=range(PASSES)):
-            for a in passes:
-                raw = ring.tile([P, PACK, P], F32, name="w1_raw", bufs=6)
+        def load_w1(b):
+            for a in range(PASSES):
+                raw = ring.tile([P, PACK, P], F32, name="w1_raw", bufs=9)
                 nc.sync.dma_start(out=raw[:], in_=w1[cols(a, K_PASS), cols(b, P)].rearrange("(p j) c -> p j c", j=PACK))
                 w1_raw[b, a] = raw
 
@@ -104,15 +110,12 @@ def tile_list_tufting_needle_page_kernel(
         def load_page(b):
             nc.sync.dma_start(out=page[b][:], in_=page0[cols(b, P), :])
 
+        idx2 = load_list("idx2", offs2)
         load_tab(0)
-        load_w1(0, range(PASSES - 1))
-        for q in range(4):
-            nc.sync.dma_start(
-                out=w2_plane[32 * q : 32 * q + 4].bitcast(I32),
-                in_=w2_scales[:, 4 * q : 4 * q + 4, :].rearrange("a r c -> r a c").bitcast(I32),
-            )
+        idx3 = load_list("idx3", offs3)
+        idx4 = load_list("idx4", offs4)
         load_tab(1)
-        load_w1(0, [PASSES - 1])
+        load_w1(0)
         w2_codes = keep.tile([P, PASSES, 2 * H], U8, name="w2_codes", align_bytes=64)
         nc.sync.dma_start(out=w2_codes[:].bitcast(I32), in_=w2_words.rearrange("a p c -> p a c").bitcast(I32))
         for a in range(PASSES):
@@ -124,10 +127,8 @@ def tile_list_tufting_needle_page_kernel(
         load_tab(2)
         wgs_sb = keep.tile([P, S], F32, name="wgs_sb")
         nc.sync.dma_start(out=wgs_sb[:], in_=wgs)
-        idx2 = load_list("idx2", offs2)
         load_page(0)
         load_w1(1)
-        idx3 = load_list("idx3", offs3)
 
         vec_ps = psum.tile([P, P], F32, name="vec_ps", tag="bank_d")
         nc.tensor.transpose(vec_ps[:], vec_rows[:], ident[:])
@@ -139,10 +140,16 @@ def tile_list_tufting_needle_page_kernel(
 
         picked = {}
         for a in range(PASSES):
-            for h in range(HALVES):
-                words = keep.tile([P, HALF], U32, name="picked%d_%d" % (a, h), align_bytes=64)
-                nc.vector.tensor_copy(out=words[:], in_=tab[a][:].indirect(half_list(idx, h)))
-                picked[a, h] = words
+            if a == 0:
+                words = shared.tile([P, S], U32, name="picked_first", align_bytes=64, offset=0)
+            else:
+                words = keep.tile([P, S], U32, name="picked%d" % a, align_bytes=64)
+            if a + 1 < PASSES:
+                nc.vector.tensor_copy(out=words[:], in_=tab[a][:].indirect(idx[:]))
+            else:
+                for h in range(HALVES):
+                    nc.vector.tensor_copy(out=words[:, cols(h, HALF)], in_=tab[a][:].indirect(half_list(idx, h)))
+            picked[a] = words
 
         def quantise(name, grouped, width):
             codes = keep.tile([P, width], U32, name=name + "_codes", align_bytes=64)
@@ -174,11 +181,11 @@ def tile_list_tufting_needle_page_kernel(
         for b in range(1, BLOCKS):
             t = keep.tile([P, S], F32, name="gw%d" % b)
             gw[b] = weigh(t[:], b, cols(0, S))
-        gw[1, 0], gw[1, 1] = gw[1][:, cols(0, HALF)], gw[1][:, cols(1, HALF)]
+            gw[b, 0], gw[b, 1] = gw[b][:, cols(0, HALF)], gw[b][:, cols(1, HALF)]
 
         spent = {}
 
-        def first_stage(b, h, act):
+        def first_stage(b, h, act, sum_a, abs_b):
             acc_a = psum.tile([P, HALF], F32, name="acc_a", tag="bank_a")
             acc_b = psum.tile([P, HALF], F32, name="acc_b", tag="bank_b")
             for a in range(PASSES):
@@ -191,17 +198,14 @@ def tile_list_tufting_needle_page_kernel(
                     for g in range(GROUPS):
                         nc.tensor.matmul_mx(
                             out=acc[:, cols(g, P)],
-                            lhsT=picked[a, h][:, cols(g, P)].bitcast(FP8X4),
+                            lhsT=picked[a][:, cols(h * GROUPS + g, P)].bitcast(FP8X4),
                             lhsT_scale=moved[a][:, cols(h * GROUPS + g, P)],
                             rhs=weight,
                             rhs_scale=weight_plane,
                             start=a == 0 and g == 0,
                             stop=a == PASSES - 1 and g == GROUPS - 1,
                         )
-            sum_a = ring.tile([P, HALF], F32, name="sum_a", tag="left", bufs=4)
-            spent[b, h] = sum_a
             nc.scalar.copy(out=sum_a[:], in_=acc_a[:])
-            abs_b = ring.tile([P, HALF], F32, name="abs_b", tag="right", bufs=4)
             nc.scalar.activation(out=abs_b[:], in_=acc_b[:], func=ACT.Abs)
             pre = psum.tile([P, HALF], F32, name="pre", tag="bank_c")
             for term, src in enumerate((sum_a, abs_b)):
@@ -212,45 +216,46 @@ def tile_list_tufting_needle_page_kernel(
                     )
             nc.scalar.activation(out=act[:, cols(h, HALF)], in_=pre[:], func=ACT.Tanh)
 
-        def scatter(b, offsets, values, weights):
-            nc.vector.tensor_tensor(page[b][:].indirect(offsets), values, weights, ALU.mult)
+        def scatter(b, h, act):
+            nc.vector.tensor_tensor(page[b][:].indirect(half_list(idx2, h)), act[:, cols(h, HALF)], gw[b, h], ALU.mult)
 
         nxt = {}
 
-        def gather_next(b):
-            if b == 0:
-                for h in range(HALVES):
-                    nc.vector.tensor_copy(out=gw[0, h], in_=page[b][:].indirect(half_list(idx4, h)))
-                    nxt[b, h] = gw[0, h]
-            else:
-                dst = gw[b ^ (b >> 1)]
-                nc.vector.tensor_copy(out=dst, in_=page[b][:].indirect(idx4[:]))
-                for h in range(HALVES):
-                    nxt[b, h] = dst[:, cols(h, HALF)]
+        def gather_next(b, dst):
+            nc.vector.tensor_copy(out=dst, in_=page[b][:].indirect(idx4[:]))
+            for h in range(HALVES):
+                nxt[b, h] = dst[:, cols(h, HALF)]
+
+        def gather_next_half(b, h, dst):
+            nc.vector.tensor_copy(out=dst, in_=page[b][:].indirect(half_list(idx4, h)))
+            nxt[b, h] = dst
 
         turned = [keep.tile([P, GROUPS, 2, P], F32, name="turned%d" % h) for h in range(HALVES)]
 
+        def turn(b, h, x_rows):
+            x_ps = psum.tile([P, HALF], BF16, name="x_ps", tag="bank_d")
+            for g in range(GROUPS):
+                nc.tensor.transpose(x_ps[:, cols(g, P)], x_rows[:, cols(g, P)], ident_bf[:])
+            nc.scalar.copy(
+                out=turned[h][:, :, :, cols(b, 32)],
+                in_=x_ps[:].bitcast(F32).rearrange("p (g q u) -> p g u q", g=GROUPS, u=2),
+            )
+
         def reread(b):
-            if b + 1 < BLOCKS:
-                holder = spent[b + 1, HALVES - 1]
-            else:
-                holder = ring.tile([P, HALF], F32, name="holder", tag="left", bufs=4)
             got = ring.tile([P, M], F32, name="got")
             if b + 1 < BLOCKS:
+                x_rows = spent[b + 1][:].bitcast(BF16)
                 nc.vector.tensor_copy(out=got[:], in_=page[b][:].indirect(idx3[:]))
+                nc.scalar.activation(out=x_rows, in_=got[:], func=ACT.Copy, scale=row_factor(1, b))
+                for h in range(HALVES):
+                    turn(b, h, x_rows[:, cols(h, HALF)])
             else:
+                x_half = ring.tile([P, HALF], BF16, name="x_half", bufs=1)
                 for h in range(HALVES):
                     nc.vector.tensor_copy(out=got[:, cols(h, HALF)], in_=page[b][:].indirect(half_list(idx3, h)))
-            for h in range(HALVES):
-                x_rows = holder[:].bitcast(BF16)[:, cols(h, HALF)]
-                nc.scalar.activation(out=x_rows, in_=got[:, cols(h, HALF)], func=ACT.Copy, scale=row_factor(1, b))
-                x_ps = psum.tile([P, HALF], BF16, name="x_ps", tag="bank_d")
-                for g in range(GROUPS):
-                    nc.tensor.transpose(x_ps[:, cols(g, P)], x_rows[:, cols(g, P)], ident_bf[:])
-                nc.scalar.copy(
-                    out=turned[h][:, :, :, cols(b, 32)],
-                    in_=x_ps[:].bitcast(F32).rearrange("p (g q u) -> p g u q", g=GROUPS, u=2),
-                )
+                for h in range(HALVES):
+                    nc.scalar.activation(out=x_half[:], in_=got[:, cols(h, HALF)], func=ACT.Copy, scale=row_factor(1, b))
+                    turn(b, h, x_half)
 
         for b in range(BLOCKS):
             if b + 2 < BLOCKS:
@@ -258,16 +263,15 @@ def tile_list_tufting_needle_page_kernel(
             if b + 1 < BLOCKS:
                 load_page(b + 1)
             act = ring.tile([P, S], F32, name="act")
-            first_stage(b, 0, act)
-            if b < 2:
-                scatter(b, half_list(idx2, 0), act[:, cols(0, HALF)], gw[b, 0])
+            left = ring.tile([P, HALF], F32, name="left", tag="left", bufs=4)
+            right = ring.tile([P, HALF], F32, name="right", tag="right", bufs=4)
+            spent[b] = right
+            first_stage(b, 0, act, left, right)
+            scatter(b, 0, act)
+            first_stage(b, 1, act, left, right)
             if b == 0:
                 gw[0, 1] = weigh(prepare_w1(1)[:, K_PASS:].bitcast(F32), 0, cols(1, HALF))
-            first_stage(b, 1, act)
-            if b < 2:
-                scatter(b, half_list(idx2, 1), act[:, cols(1, HALF)], gw[b, 1])
-            else:
-                scatter(b, idx2[:], act[:], gw[b])
+            scatter(b, 1, act)
             if b + 2 < BLOCKS:
                 prepare_w1(b + 2)
             if b > 0:
@@ -282,7 +286,6 @@ def tile_list_tufting_needle_page_kernel(
                 out=w3_plane[32 * q : 32 * q + 4, :].bitcast(I32),
                 in_=w3_scales[0, 4 * q : 4 * q + 4, :].bitcast(I32),
             )
-        idx4 = load_list("idx4", offs4)
         w4_grouped = ring.tile([P, H * PACK], BF16, name="w4_grouped", tag="abs_x", align_bytes=64)
         w4_codes, w4_plane = quantise_weight("w4", w4_raw, w4_grouped[:], H)
 
@@ -305,7 +308,10 @@ def tile_list_tufting_needle_page_kernel(
             for pair in range(2):
                 part = cols(pair, PACK * HALF // 2)
                 nc.scalar.activation(out=abs_grouped[:, part], in_=x_grouped[:, part], func=ACT.Abs)
-            return quantise("x%d" % h, x_grouped, HALF), quantise("abs_x%d" % h, abs_grouped, HALF)
+            quantised = quantise("x%d" % h, x_grouped, HALF), quantise("abs_x%d" % h, abs_grouped, HALF)
+            if h == 1:
+                gather_next_half(0, 1, abs_grouped[:, PACK * HALF // 2 :].bitcast(F32))
+            return quantised
 
         lows = {}
 
@@ -336,8 +342,10 @@ def tile_list_tufting_needle_page_kernel(
             finish(BLOCKS - 1, h)
 
         reread(BLOCKS - 1)
-        for b in range(BLOCKS):
-            gather_next(b)
+        gather_next_half(0, 0, gw[0, 0])
+        gather_next(1, act[:])
+        gather_next(2, gw[3])
+        gather_next(3, gw[2])
         first_q = quantise_x(0, turn_back(0))
         x_later = turn_back(1)
         second_stage(0, *first_q)

@@ -18,17 +18,24 @@ ACT = mybir.ActivationFunctionType
 ALU = mybir.AluOpType
 
 P = 128
+QUADRANT = 32
+QUADRANTS = P // QUADRANT
+SCALE_ROWS = 4
 PACK = 4
 K_PASS = P * PACK
 PASSES = K // K_PASS
+LAST_PASS = PASSES - 1
 BLOCKS = H // P
+LAST_BLOCK = BLOCKS - 1
 HALF = 512
 HALVES = S // HALF
 GROUPS = HALF // P
 LIST_COLS = HALF // 16
-LIVE_ROWS = 100
-SPARE_ROWS = 32 - 4 * PASSES
-VEC_ROW = P - 3 * BLOCKS
+SPARE_ROWS = QUADRANT - SCALE_ROWS * PASSES
+PLANE_ROWS = (QUADRANTS - 1) * QUADRANT + SCALE_ROWS
+FACTORS = 3
+FACTOR_ROW = P - FACTORS * BLOCKS
+GAIN, SC, GV = range(FACTORS)
 
 
 def tile_list_tufting_needle_page_kernel(
@@ -46,52 +53,54 @@ def tile_list_tufting_needle_page_kernel(
             return slice(i * width, (i + 1) * width)
 
         def load_list(name, src):
-            lst = keep.tile([P, S // 16], U16, name=name)
-            nc.sync.dma_start(lst[:], src)
-            return lst
+            offsets = keep.tile([P, S // 16], U16, name=name)
+            nc.sync.dma_start(offsets[:], src)
+            return offsets
 
-        def half_list(lst, h):
-            return lst[:, cols(h, LIST_COLS)]
+        def half_list(offsets, h):
+            return offsets[:, cols(h, LIST_COLS)]
 
-        def zeroed_bytes(engine, name, shape):
-            t = keep.tile(shape, U8, name=name, align_bytes=64)
-            engine.memset(t[:].bitcast(I32), 0)
-            return t
+        def zeroed_plane(engine, name, shape):
+            plane = keep.tile(shape, U8, name=name, align_bytes=64)
+            engine.memset(plane[:].bitcast(I32), 0)
+            return plane
+
+        def quadrant_rows(q):
+            return slice(QUADRANT * q, QUADRANT * q + SCALE_ROWS)
 
         ident = keep.tile([P, P], F32, name="ident")
         make_identity(nc, ident[:])
         ident_bf = keep.tile([P, P], BF16, name="ident_bf")
         make_identity(nc, ident_bf[:])
-        w2_plane = zeroed_bytes(nc.vector, "w2_plane", [P, PASSES, H])
+        w2_plane = zeroed_plane(nc.vector, "w2_plane", [P, PASSES, H])
+
         scale_window = shared.tile([P, T], U8, name="scale_window", offset=2 * S)
-        for q in range(4):
-            nc.vector.memset(scale_window[32 * q : 32 * q + SPARE_ROWS, :].bitcast(I32), 0)
+        for q in range(QUADRANTS):
+            nc.vector.memset(scale_window[QUADRANT * q : QUADRANT * q + SPARE_ROWS, :].bitcast(I32), 0)
             nc.scalar.dma_start(
-                out=scale_window[32 * q + SPARE_ROWS : 32 * (q + 1), :].bitcast(I32),
-                in_=tab_scales[:, 4 * q : 4 * q + 4, :].bitcast(I32),
+                out=scale_window[QUADRANT * q + SPARE_ROWS : QUADRANT * (q + 1), :].bitcast(I32),
+                in_=tab_scales[:, cols(q, SCALE_ROWS), :].bitcast(I32),
             )
         idx = load_list("idx", offs)
-        moved = [zeroed_bytes(nc.gpsimd, "moved%d" % a, [P, S]) for a in range(PASSES)]
+        tab_plane = [zeroed_plane(nc.gpsimd, "tab_plane%d" % a, [P, S]) for a in range(PASSES)]
         picked_scales = keep.tile([P, S], U8, name="picked_scales", align_bytes=64)
         nc.vector.tensor_copy(out=picked_scales[:], in_=scale_window[:].indirect(idx[:]))
-        for q in range(4):
+        for q in range(QUADRANTS):
             nc.gpsimd.dma_start(
-                out=w2_plane[32 * q : 32 * q + 4].bitcast(I32),
-                in_=w2_scales[:, 4 * q : 4 * q + 4, :].rearrange("a r c -> r a c").bitcast(I32),
+                out=w2_plane[quadrant_rows(q)].bitcast(I32),
+                in_=w2_scales[:, cols(q, SCALE_ROWS), :].rearrange("a r c -> r a c").bitcast(I32),
             )
-        vec_rows = keep.tile([P, P], F32, name="vec_rows")
-        nc.gpsimd.memset(vec_rows[:VEC_ROW, :], 0.0)
-        for i, src in enumerate((gain, sc, gv)):
-            nc.gpsimd.dma_start(
-                out=vec_rows[VEC_ROW + i * BLOCKS : VEC_ROW + (i + 1) * BLOCKS, :],
-                in_=src.rearrange("(b c) -> b c", c=P),
-            )
-        warm = keep.tile([P, 1], F32, name="warm")
-        nc.vector.memset(warm[:], 0.0)
-        nc.scalar.activation(out=warm[:], in_=warm[:], func=ACT.Tanh)
-        w3_plane = zeroed_bytes(nc.vector, "w3_plane", [P, H])
 
-        tab = [keep.tile([P, T], U32, name="tab%d" % a) for a in range(PASSES - 1)]
+        factor_rows = keep.tile([P, P], F32, name="factor_rows")
+        nc.gpsimd.memset(factor_rows[:FACTOR_ROW, :], 0.0)
+        for i, vector in enumerate((gain, sc, gv)):
+            nc.gpsimd.dma_start(
+                out=factor_rows[FACTOR_ROW + i * BLOCKS : FACTOR_ROW + (i + 1) * BLOCKS, :],
+                in_=vector.rearrange("(b c) -> b c", c=P),
+            )
+        w3_plane = zeroed_plane(nc.vector, "w3_plane", [P, H])
+
+        tab = [keep.tile([P, T], U32, name="tab%d" % a) for a in range(LAST_PASS)]
         tab.append(shared.tile([P, T], U32, name="tab_last", offset=4 * S))
 
         def load_tab(a):
@@ -101,7 +110,7 @@ def tile_list_tufting_needle_page_kernel(
 
         def load_w1(b):
             for a in range(PASSES):
-                raw = ring.tile([P, PACK, P], F32, name="w1_raw", bufs=9)
+                raw = ring.tile([P, PACK, P], F32, name="w1_raw", bufs=3 * PASSES)
                 nc.sync.dma_start(out=raw[:], in_=w1[cols(a, K_PASS), cols(b, P)].rearrange("(p j) c -> p j c", j=PACK))
                 w1_raw[b, a] = raw
 
@@ -119,37 +128,33 @@ def tile_list_tufting_needle_page_kernel(
         w2_codes = keep.tile([P, PASSES, 2 * H], U8, name="w2_codes", align_bytes=64)
         nc.sync.dma_start(out=w2_codes[:].bitcast(I32), in_=w2_words.rearrange("a p c -> p a c").bitcast(I32))
         for a in range(PASSES):
-            first_row = SPARE_ROWS + 4 * a
+            first_row = SPARE_ROWS + SCALE_ROWS * a
             nc.sync.dma_start(
-                out=moved[a][:LIVE_ROWS, :].bitcast(I32),
-                in_=picked_scales[first_row : first_row + LIVE_ROWS, :].bitcast(I32),
+                out=tab_plane[a][:PLANE_ROWS, :].bitcast(I32),
+                in_=picked_scales[first_row : first_row + PLANE_ROWS, :].bitcast(I32),
             )
-        load_tab(2)
+        load_tab(LAST_PASS)
         wgs_sb = keep.tile([P, S], F32, name="wgs_sb")
         nc.sync.dma_start(out=wgs_sb[:], in_=wgs)
         load_page(0)
         load_w1(1)
 
-        vec_ps = psum.tile([P, P], F32, name="vec_ps", tag="bank_d")
-        nc.tensor.transpose(vec_ps[:], vec_rows[:], ident[:])
-        vec = keep.tile([P, 3 * BLOCKS], F32, name="vec")
-        nc.scalar.copy(out=vec[:], in_=vec_ps[:, VEC_ROW:])
+        factors_ps = psum.tile([P, P], F32, name="factors_ps", tag="bank_d")
+        nc.tensor.transpose(factors_ps[:], factor_rows[:], ident[:])
+        factors = keep.tile([P, FACTORS * BLOCKS], F32, name="factors")
+        nc.scalar.copy(out=factors[:], in_=factors_ps[:, FACTOR_ROW:])
 
-        def row_factor(i, b):
-            return vec[:, i * BLOCKS + b : i * BLOCKS + b + 1]
+        def row_factor(which, b):
+            return factors[:, which * BLOCKS + b : which * BLOCKS + b + 1]
 
-        picked = {}
-        for a in range(PASSES):
-            if a == 0:
-                words = shared.tile([P, S], U32, name="picked_first", align_bytes=64, offset=0)
-            else:
-                words = keep.tile([P, S], U32, name="picked%d" % a, align_bytes=64)
-            if a + 1 < PASSES:
-                nc.vector.tensor_copy(out=words[:], in_=tab[a][:].indirect(idx[:]))
-            else:
-                for h in range(HALVES):
-                    nc.vector.tensor_copy(out=words[:, cols(h, HALF)], in_=tab[a][:].indirect(half_list(idx, h)))
-            picked[a] = words
+        picked = [shared.tile([P, S], U32, name="picked_first", align_bytes=64, offset=0)]
+        picked.extend([keep.tile([P, S], U32, name="picked%d" % a, align_bytes=64) for a in range(1, PASSES)])
+        for a in range(LAST_PASS):
+            nc.vector.tensor_copy(out=picked[a][:], in_=tab[a][:].indirect(idx[:]))
+        for h in range(HALVES):
+            nc.vector.tensor_copy(
+                out=picked[LAST_PASS][:, cols(h, HALF)], in_=tab[LAST_PASS][:].indirect(half_list(idx, h))
+            )
 
         def quantise(name, grouped, width):
             codes = keep.tile([P, width], U32, name=name + "_codes", align_bytes=64)
@@ -157,33 +162,36 @@ def tile_list_tufting_needle_page_kernel(
             nc.vector.quantize_mx(out=codes[:].bitcast(FP8X4), scales=plane[:], in_=grouped)
             return codes, plane
 
-        def quantise_weight(name, raw, grouped, width):
+        def interleave(grouped, raw):
             nc.scalar.copy(out=grouped.rearrange("p (c j) -> p c j", j=PACK), in_=raw[:].rearrange("p j c -> p c j"))
-            return quantise(name, grouped, width)
 
         w1_q = {}
 
         def prepare_w1(b):
-            grouped = ring.tile([P, PASSES * K_PASS], BF16, name="w1_grouped", align_bytes=64, bufs=4)
+            grouped = ring.tile([P, PASSES * K_PASS], BF16, name="w1_grouped", align_bytes=64, bufs=BLOCKS)
             for a in range(PASSES):
-                w1_q[b, a] = quantise_weight("w1_%d_%d" % (b, a), w1_raw[b, a], grouped[:, cols(a, K_PASS)], P)
+                interleave(grouped[:, cols(a, K_PASS)], w1_raw[b, a])
+            codes, plane = quantise("w1_%d" % b, grouped[:, : LAST_PASS * K_PASS], LAST_PASS * P)
+            for a in range(LAST_PASS):
+                w1_q[b, a] = codes[:, cols(a, P)], plane[:, cols(a, P)]
+            codes, plane = quantise("w1_%d_last" % b, grouped[:, LAST_PASS * K_PASS :], P)
+            w1_q[b, LAST_PASS] = codes[:], plane[:]
             return grouped
 
         prepare_w1(0)
-        gw = {}
 
         def weigh(dst, b, entries):
-            nc.vector.tensor_scalar(dst, wgs_sb[:, entries], row_factor(0, b), None, ALU.mult)
+            nc.vector.tensor_scalar(dst, wgs_sb[:, entries], row_factor(GAIN, b), None, ALU.mult)
             return dst
 
-        gw_first = keep.tile([P, HALF], F32, name="gw_first")
-        gw[0, 0] = weigh(gw_first[:], 0, cols(0, HALF))
+        first_weights = keep.tile([P, HALF], F32, name="first_weights")
+        half_weights = {(0, 0): weigh(first_weights[:], 0, cols(0, HALF))}
+        block_weights = {}
         for b in range(1, BLOCKS):
-            t = keep.tile([P, S], F32, name="gw%d" % b)
-            gw[b] = weigh(t[:], b, cols(0, S))
-            gw[b, 0], gw[b, 1] = gw[b][:, cols(0, HALF)], gw[b][:, cols(1, HALF)]
-
-        spent = {}
+            weights = keep.tile([P, S], F32, name="weights%d" % b)
+            block_weights[b] = weigh(weights[:], b, cols(0, S))
+            for h in range(HALVES):
+                half_weights[b, h] = weights[:, cols(h, HALF)]
 
         def first_stage(b, h, act, sum_a, abs_b):
             acc_a = psum.tile([P, HALF], F32, name="acc_a", tag="bank_a")
@@ -191,7 +199,7 @@ def tile_list_tufting_needle_page_kernel(
             for a in range(PASSES):
                 codes, plane = w1_q[b, a]
                 moving = (
-                    (acc_a, codes[:].bitcast(FP8X4), plane[:]),
+                    (acc_a, codes.bitcast(FP8X4), plane),
                     (acc_b, w2_codes[:, a, cols(b, 2 * P)].bitcast(FP4X4), w2_plane[:, a, cols(b, P)]),
                 )
                 for acc, weight, weight_plane in moving:
@@ -199,11 +207,11 @@ def tile_list_tufting_needle_page_kernel(
                         nc.tensor.matmul_mx(
                             out=acc[:, cols(g, P)],
                             lhsT=picked[a][:, cols(h * GROUPS + g, P)].bitcast(FP8X4),
-                            lhsT_scale=moved[a][:, cols(h * GROUPS + g, P)],
+                            lhsT_scale=tab_plane[a][:, cols(h * GROUPS + g, P)],
                             rhs=weight,
                             rhs_scale=weight_plane,
                             start=a == 0 and g == 0,
-                            stop=a == PASSES - 1 and g == GROUPS - 1,
+                            stop=a == LAST_PASS and g == GROUPS - 1,
                         )
             nc.scalar.copy(out=sum_a[:], in_=acc_a[:])
             nc.scalar.activation(out=abs_b[:], in_=acc_b[:], func=ACT.Abs)
@@ -216,8 +224,77 @@ def tile_list_tufting_needle_page_kernel(
                     )
             nc.scalar.activation(out=act[:, cols(h, HALF)], in_=pre[:], func=ACT.Tanh)
 
-        def scatter(b, h, act):
-            nc.vector.tensor_tensor(page[b][:].indirect(half_list(idx2, h)), act[:, cols(h, HALF)], gw[b, h], ALU.mult)
+        def scatter(b, offsets, values, weights):
+            nc.vector.tensor_tensor(page[b][:].indirect(offsets), values, weights, ALU.mult)
+
+        def scatter_half(b, h, act):
+            scatter(b, half_list(idx2, h), act[:, cols(h, HALF)], half_weights[b, h])
+
+        turned = [keep.tile([P, GROUPS, 2, P], F32, name="turned%d" % h) for h in range(HALVES)]
+
+        def turn(b, h, x_rows):
+            x_ps = psum.tile([P, HALF], BF16, name="x_ps", tag="bank_d")
+            for g in range(GROUPS):
+                nc.tensor.transpose(x_ps[:, cols(g, P)], x_rows[:, cols(g, P)], ident_bf[:])
+            nc.scalar.copy(
+                out=turned[h][:, :, :, cols(b, P // PACK)],
+                in_=x_ps[:].bitcast(F32).rearrange("p (g q u) -> p g u q", g=GROUPS, u=2),
+            )
+
+        def reread(b, holder):
+            got = ring.tile([P, M], F32, name="got")
+            x_rows = holder[:].bitcast(BF16)
+            nc.vector.tensor_copy(out=got[:], in_=page[b][:].indirect(idx3[:]))
+            nc.scalar.activation(out=x_rows, in_=got[:], func=ACT.Copy, scale=row_factor(SC, b))
+            for h in range(HALVES):
+                turn(b, h, x_rows[:, cols(h, HALF)])
+
+        def reread_last():
+            got = ring.tile([P, M], F32, name="got")
+            x_half = ring.tile([P, HALF], BF16, name="x_half", bufs=1)
+            for h in range(HALVES):
+                nc.vector.tensor_copy(out=got[:, cols(h, HALF)], in_=page[LAST_BLOCK][:].indirect(half_list(idx3, h)))
+            for h in range(HALVES):
+                nc.scalar.activation(
+                    out=x_half[:], in_=got[:, cols(h, HALF)], func=ACT.Copy, scale=row_factor(SC, LAST_BLOCK)
+                )
+                turn(LAST_BLOCK, h, x_half)
+
+        for b in range(BLOCKS):
+            if b + 2 < BLOCKS:
+                load_w1(b + 2)
+            if b + 1 < BLOCKS:
+                load_page(b + 1)
+            act = ring.tile([P, S], F32, name="act")
+            sum_a = ring.tile([P, HALF], F32, name="sum_a", tag="left", bufs=BLOCKS)
+            abs_b = ring.tile([P, HALF], F32, name="abs_b", tag="right", bufs=BLOCKS)
+            first_stage(b, 0, act, sum_a, abs_b)
+            if b < LAST_BLOCK:
+                scatter_half(b, 0, act)
+            first_stage(b, 1, act, sum_a, abs_b)
+            if b == 0:
+                half_weights[0, 1] = weigh(prepare_w1(1)[:, K_PASS:].bitcast(F32), 0, cols(1, HALF))
+            if b < LAST_BLOCK:
+                scatter_half(b, 1, act)
+            else:
+                scatter(b, idx2[:], act[:], block_weights[b])
+            if b + 2 < BLOCKS:
+                prepare_w1(b + 2)
+            if b > 0:
+                reread(b - 1, abs_b)
+
+        w4_raw = keep.tile([P, PACK, H], F32, name="w4_raw")
+        nc.sync.dma_start(out=w4_raw[:], in_=w4.rearrange("(p j) c -> p j c", j=PACK))
+        w3_codes = keep.tile([P, 2 * H], U8, name="w3_codes", align_bytes=64)
+        nc.sync.dma_start(out=w3_codes[:].bitcast(I32), in_=w3_words[0].bitcast(I32))
+        for q in range(QUADRANTS):
+            nc.sync.dma_start(
+                out=w3_plane[quadrant_rows(q), :].bitcast(I32),
+                in_=w3_scales[0, cols(q, SCALE_ROWS), :].bitcast(I32),
+            )
+        w4_grouped = ring.tile([P, H * PACK], BF16, name="w4_grouped", tag="abs_x", align_bytes=64)
+        interleave(w4_grouped[:], w4_raw)
+        w4_codes, w4_plane = quantise("w4", w4_grouped[:], H)
 
         nxt = {}
 
@@ -229,65 +306,6 @@ def tile_list_tufting_needle_page_kernel(
         def gather_next_half(b, h, dst):
             nc.vector.tensor_copy(out=dst, in_=page[b][:].indirect(half_list(idx4, h)))
             nxt[b, h] = dst
-
-        turned = [keep.tile([P, GROUPS, 2, P], F32, name="turned%d" % h) for h in range(HALVES)]
-
-        def turn(b, h, x_rows):
-            x_ps = psum.tile([P, HALF], BF16, name="x_ps", tag="bank_d")
-            for g in range(GROUPS):
-                nc.tensor.transpose(x_ps[:, cols(g, P)], x_rows[:, cols(g, P)], ident_bf[:])
-            nc.scalar.copy(
-                out=turned[h][:, :, :, cols(b, 32)],
-                in_=x_ps[:].bitcast(F32).rearrange("p (g q u) -> p g u q", g=GROUPS, u=2),
-            )
-
-        def reread(b):
-            got = ring.tile([P, M], F32, name="got")
-            if b + 1 < BLOCKS:
-                x_rows = spent[b + 1][:].bitcast(BF16)
-                nc.vector.tensor_copy(out=got[:], in_=page[b][:].indirect(idx3[:]))
-                nc.scalar.activation(out=x_rows, in_=got[:], func=ACT.Copy, scale=row_factor(1, b))
-                for h in range(HALVES):
-                    turn(b, h, x_rows[:, cols(h, HALF)])
-            else:
-                x_half = ring.tile([P, HALF], BF16, name="x_half", bufs=1)
-                for h in range(HALVES):
-                    nc.vector.tensor_copy(out=got[:, cols(h, HALF)], in_=page[b][:].indirect(half_list(idx3, h)))
-                for h in range(HALVES):
-                    nc.scalar.activation(out=x_half[:], in_=got[:, cols(h, HALF)], func=ACT.Copy, scale=row_factor(1, b))
-                    turn(b, h, x_half)
-
-        for b in range(BLOCKS):
-            if b + 2 < BLOCKS:
-                load_w1(b + 2)
-            if b + 1 < BLOCKS:
-                load_page(b + 1)
-            act = ring.tile([P, S], F32, name="act")
-            left = ring.tile([P, HALF], F32, name="left", tag="left", bufs=4)
-            right = ring.tile([P, HALF], F32, name="right", tag="right", bufs=4)
-            spent[b] = right
-            first_stage(b, 0, act, left, right)
-            scatter(b, 0, act)
-            first_stage(b, 1, act, left, right)
-            if b == 0:
-                gw[0, 1] = weigh(prepare_w1(1)[:, K_PASS:].bitcast(F32), 0, cols(1, HALF))
-            scatter(b, 1, act)
-            if b + 2 < BLOCKS:
-                prepare_w1(b + 2)
-            if b > 0:
-                reread(b - 1)
-
-        w4_raw = keep.tile([P, PACK, H], F32, name="w4_raw")
-        nc.sync.dma_start(out=w4_raw[:], in_=w4.rearrange("(p j) c -> p j c", j=PACK))
-        w3_codes = keep.tile([P, 2 * H], U8, name="w3_codes", align_bytes=64)
-        nc.sync.dma_start(out=w3_codes[:].bitcast(I32), in_=w3_words[0].bitcast(I32))
-        for q in range(4):
-            nc.sync.dma_start(
-                out=w3_plane[32 * q : 32 * q + 4, :].bitcast(I32),
-                in_=w3_scales[0, 4 * q : 4 * q + 4, :].bitcast(I32),
-            )
-        w4_grouped = ring.tile([P, H * PACK], BF16, name="w4_grouped", tag="abs_x", align_bytes=64)
-        w4_codes, w4_plane = quantise_weight("w4", w4_raw, w4_grouped[:], H)
 
         def turn_back(h):
             x_words = ring.tile([P, HALF, 2], F32, name="x_words", align_bytes=64)
@@ -303,24 +321,18 @@ def tile_list_tufting_needle_page_kernel(
             return x_words[:].rearrange("p m u -> p (m u)").bitcast(BF16)
 
         def quantise_x(h, x_grouped):
-            abs_x = ring.tile([P, HALF, PACK], BF16, name="abs_x", tag="abs_x", align_bytes=64)
-            abs_grouped = abs_x[:].rearrange("p m j -> p (m j)")
-            for pair in range(2):
-                part = cols(pair, PACK * HALF // 2)
-                nc.scalar.activation(out=abs_grouped[:, part], in_=x_grouped[:, part], func=ACT.Abs)
-            quantised = quantise("x%d" % h, x_grouped, HALF), quantise("abs_x%d" % h, abs_grouped, HALF)
-            if h == 1:
-                gather_next_half(0, 1, abs_grouped[:, PACK * HALF // 2 :].bitcast(F32))
-            return quantised
+            abs_x = ring.tile([P, HALF * PACK], BF16, name="abs_x", tag="abs_x", align_bytes=64)
+            for part in range(2):
+                span = cols(part, PACK * HALF // 2)
+                nc.scalar.activation(out=abs_x[:, span], in_=x_grouped[:, span], func=ACT.Abs)
+            return quantise("x%d" % h, x_grouped, HALF), quantise("abs_x%d" % h, abs_x[:], HALF), abs_x
 
-        lows = {}
-
-        def finish(b, h):
-            low = lows[b, h]
-            nc.vector.scalar_tensor_tensor(low[:], low[:], row_factor(2, b), nxt[b, h], ALU.mult, ALU.mult)
+        def finish(b, h, low):
+            nc.vector.scalar_tensor_tensor(low[:], low[:], row_factor(GV, b), nxt[b, h], ALU.mult, ALU.mult)
             nc.sync.dma_start(out=out[cols(b, P), cols(h, HALF)], in_=low[:])
 
         def second_stage(h, x_q, abs_q):
+            lows = []
             for b in range(BLOCKS):
                 y3 = psum.tile([P, HALF], F32, name="y3", tag="bank_a")
                 y4 = psum.tile([P, HALF], F32, name="y4", tag="bank_b")
@@ -332,21 +344,23 @@ def tile_list_tufting_needle_page_kernel(
                     out=y4[:], lhsT=w4_codes[:, cols(b, P)].bitcast(FP8X4), lhsT_scale=w4_plane[:, cols(b, P)],
                     rhs=abs_q[0][:].bitcast(FP8X4), rhs_scale=abs_q[1][:], start=True, stop=True,
                 )
-                y3_sb = ring.tile([P, HALF], F32, name="y3_sb", tag="left", bufs=4)
+                y3_sb = ring.tile([P, HALF], F32, name="y3_sb", tag="left", bufs=BLOCKS)
                 nc.scalar.copy(out=y3_sb[:], in_=y3[:])
-                low = ring.tile([P, HALF], F32, name="low", tag="right", bufs=4)
+                low = ring.tile([P, HALF], F32, name="low", tag="right", bufs=BLOCKS)
                 nc.vector.tensor_tensor(low[:], y4[:], y3_sb[:], ALU.min)
-                lows[b, h] = low
+                lows.append(low)
                 if b > 0:
-                    finish(b - 1, h)
-            finish(BLOCKS - 1, h)
+                    finish(b - 1, h, lows[b - 1])
+            finish(LAST_BLOCK, h, lows[LAST_BLOCK])
 
-        reread(BLOCKS - 1)
-        gather_next_half(0, 0, gw[0, 0])
+        reread_last()
+        gather_next_half(0, 0, half_weights[0, 0])
         gather_next(1, act[:])
-        gather_next(2, gw[3])
-        gather_next(3, gw[2])
-        first_q = quantise_x(0, turn_back(0))
+        gather_next(2, block_weights[3])
+        gather_next(3, block_weights[2])
+        first_q = quantise_x(0, turn_back(0))[:2]
         x_later = turn_back(1)
         second_stage(0, *first_q)
-        second_stage(1, *quantise_x(1, x_later))
+        later_x_q, later_abs_q, later_abs_x = quantise_x(1, x_later)
+        gather_next_half(0, 1, later_abs_x[:, PACK * HALF // 2 :].bitcast(F32))
+        second_stage(1, later_x_q, later_abs_q)

from contextlib import ExitStack

import concourse.mybir as mybir
from concourse.masks import make_identity

K, H, T, S, T2, M = 1536, 512, 4096, 1024, 2048, 1024
FLOPS = 2 * (2 * K * H * S + 2 * H * H * M)

F32 = mybir.dt.float32
BF16 = mybir.dt.bfloat16
I32 = mybir.dt.int32
U32 = mybir.dt.uint32
U16 = mybir.dt.uint16
U8 = mybir.dt.uint8
FP8X4 = mybir.dt.float8_e4m3fn_x4
FP4X4 = mybir.dt.float4_e2m1fn_x4
ACT = mybir.ActivationFunctionType
ALU = mybir.AluOpType

P = 128
QUADRANT = 32
QUADRANTS = P // QUADRANT
SCALE_ROWS = 4
PACK = 4
K_PASS = P * PACK
PASSES = K // K_PASS
LAST_PASS = PASSES - 1
BLOCKS = H // P
LAST_BLOCK = BLOCKS - 1
HALF = 512
HALVES = S // HALF
GROUPS = HALF // P
LIST_COLS = HALF // 16
SPARE_ROWS = QUADRANT - SCALE_ROWS * PASSES
PLANE_ROWS = (QUADRANTS - 1) * QUADRANT + SCALE_ROWS
FACTORS = 3
FACTOR_ROW = P - FACTORS * BLOCKS
GAIN, SC, GV = range(FACTORS)


def tile_list_tufting_needle_page_kernel(
    tc, tab_words, tab_scales, offs, w1, w2_words, w2_scales, gain, page0, offs2, wgs, offs3, offs4, sc,
    w3_words, w3_scales, w4, gv, out,
):
    nc = tc.nc
    with ExitStack() as ctx:
        keep = ctx.enter_context(tc.tile_pool(name="keep", bufs=1))
        shared = ctx.enter_context(tc.tile_pool(name="shared", bufs=1))
        ring = ctx.enter_context(tc.tile_pool(name="ring", bufs=2))
        psum = ctx.enter_context(tc.psum_pool(name="psum", bufs=2))

        def cols(i, width):
            return slice(i * width, (i + 1) * width)

        def load_list(name, src):
            offsets = keep.tile([P, S // 16], U16, name=name)
            nc.sync.dma_start(offsets[:], src)
            return offsets

        def half_list(offsets, h):
            return offsets[:, cols(h, LIST_COLS)]

        def zeroed_plane(engine, name, shape):
            plane = keep.tile(shape, U8, name=name, align_bytes=64)
            engine.memset(plane[:].bitcast(I32), 0)
            return plane

        def quadrant_rows(q):
            return slice(QUADRANT * q, QUADRANT * q + SCALE_ROWS)

        ident = keep.tile([P, P], F32, name="ident")
        make_identity(nc, ident[:])
        ident_bf = keep.tile([P, P], BF16, name="ident_bf")
        make_identity(nc, ident_bf[:])
        w2_plane = zeroed_plane(nc.vector, "w2_plane", [P, PASSES, H])

        scale_window = shared.tile([P, T], U8, name="scale_window", offset=2 * S)
        for q in range(QUADRANTS):
            nc.vector.memset(scale_window[QUADRANT * q : QUADRANT * q + SPARE_ROWS, :].bitcast(I32), 0)
            nc.scalar.dma_start(
                out=scale_window[QUADRANT * q + SPARE_ROWS : QUADRANT * (q + 1), :].bitcast(I32),
                in_=tab_scales[:, cols(q, SCALE_ROWS), :].bitcast(I32),
            )
        idx = load_list("idx", offs)
        tab_plane = [zeroed_plane(nc.gpsimd, "tab_plane%d" % a, [P, S]) for a in range(PASSES)]
        picked_scales = keep.tile([P, S], U8, name="picked_scales", align_bytes=64)
        nc.vector.tensor_copy(out=picked_scales[:], in_=scale_window[:].indirect(idx[:]))
        for q in range(QUADRANTS):
            nc.gpsimd.dma_start(
                out=w2_plane[quadrant_rows(q)].bitcast(I32),
                in_=w2_scales[:, cols(q, SCALE_ROWS), :].rearrange("a r c -> r a c").bitcast(I32),
            )

        factor_rows = keep.tile([P, P], F32, name="factor_rows")
        nc.gpsimd.memset(factor_rows[:FACTOR_ROW, :], 0.0)
        for i, vector in enumerate((gain, sc, gv)):
            nc.gpsimd.dma_start(
                out=factor_rows[FACTOR_ROW + i * BLOCKS : FACTOR_ROW + (i + 1) * BLOCKS, :],
                in_=vector.rearrange("(b c) -> b c", c=P),
            )
        w3_plane = zeroed_plane(nc.vector, "w3_plane", [P, H])

        tab = [keep.tile([P, T], U32, name="tab%d" % a) for a in range(LAST_PASS)]
        tab.append(shared.tile([P, T], U32, name="tab_last", offset=4 * S))

        def load_tab(a):
            nc.sync.dma_start(out=tab[a][:].bitcast(I32), in_=tab_words[a].rearrange("p t i -> p (t i)").bitcast(I32))

        w1_raw = {}

        def load_w1(b):
            for a in range(PASSES):
                raw = ring.tile([P, PACK, P], F32, name="w1_raw", bufs=3 * PASSES)
                nc.sync.dma_start(out=raw[:], in_=w1[cols(a, K_PASS), cols(b, P)].rearrange("(p j) c -> p j c", j=PACK))
                w1_raw[b, a] = raw

        page = [keep.tile([P, T2], F32, name="page%d" % b) for b in range(BLOCKS)]

        def load_page(b):
            nc.sync.dma_start(out=page[b][:], in_=page0[cols(b, P), :])

        idx2 = load_list("idx2", offs2)
        load_tab(0)
        idx3 = load_list("idx3", offs3)
        idx4 = load_list("idx4", offs4)
        load_tab(1)
        load_w1(0)
        w2_codes = keep.tile([P, PASSES, 2 * H], U8, name="w2_codes", align_bytes=64)
        nc.sync.dma_start(out=w2_codes[:].bitcast(I32), in_=w2_words.rearrange("a p c -> p a c").bitcast(I32))
        for a in range(PASSES):
            first_row = SPARE_ROWS + SCALE_ROWS * a
            nc.sync.dma_start(
                out=tab_plane[a][:PLANE_ROWS, :].bitcast(I32),
                in_=picked_scales[first_row : first_row + PLANE_ROWS, :].bitcast(I32),
            )
        load_tab(LAST_PASS)
        wgs_sb = keep.tile([P, S], F32, name="wgs_sb")
        nc.sync.dma_start(out=wgs_sb[:], in_=wgs)
        load_page(0)
        load_w1(1)

        factors_ps = psum.tile([P, P], F32, name="factors_ps", tag="bank_d")
        nc.tensor.transpose(factors_ps[:], factor_rows[:], ident[:])
        factors = keep.tile([P, FACTORS * BLOCKS], F32, name="factors")
        nc.scalar.copy(out=factors[:], in_=factors_ps[:, FACTOR_ROW:])

        def row_factor(which, b):
            return factors[:, which * BLOCKS + b : which * BLOCKS + b + 1]

        picked = [shared.tile([P, S], U32, name="picked_first", align_bytes=64, offset=0)]
        picked.extend([keep.tile([P, S], U32, name="picked%d" % a, align_bytes=64) for a in range(1, PASSES)])
        for a in range(LAST_PASS):
            nc.vector.tensor_copy(out=picked[a][:], in_=tab[a][:].indirect(idx[:]))
        for h in range(HALVES):
            nc.vector.tensor_copy(
                out=picked[LAST_PASS][:, cols(h, HALF)], in_=tab[LAST_PASS][:].indirect(half_list(idx, h))
            )

        def quantise(name, grouped, width):
            codes = keep.tile([P, width], U32, name=name + "_codes", align_bytes=64)
            plane = keep.tile([P, width], U8, name=name + "_plane", align_bytes=64)
            nc.vector.quantize_mx(out=codes[:].bitcast(FP8X4), scales=plane[:], in_=grouped)
            return codes, plane

        def interleave(grouped, raw):
            nc.scalar.copy(out=grouped.rearrange("p (c j) -> p c j", j=PACK), in_=raw[:].rearrange("p j c -> p c j"))

        w1_q = {}

        def prepare_w1(b):
            grouped = ring.tile([P, PASSES * K_PASS], BF16, name="w1_grouped", align_bytes=64, bufs=BLOCKS)
            for a in range(PASSES):
                interleave(grouped[:, cols(a, K_PASS)], w1_raw[b, a])
            codes, plane = quantise("w1_%d" % b, grouped[:, : LAST_PASS * K_PASS], LAST_PASS * P)
            for a in range(LAST_PASS):
                w1_q[b, a] = codes[:, cols(a, P)], plane[:, cols(a, P)]
            codes, plane = quantise("w1_%d_last" % b, grouped[:, LAST_PASS * K_PASS :], P)
            w1_q[b, LAST_PASS] = codes[:], plane[:]
            return grouped

        prepare_w1(0)

        def weigh(dst, b, entries):
            nc.vector.tensor_scalar(dst, wgs_sb[:, entries], row_factor(GAIN, b), None, ALU.mult)
            return dst

        first_weights = keep.tile([P, HALF], F32, name="first_weights")
        half_weights = {(0, 0): weigh(first_weights[:], 0, cols(0, HALF))}
        block_weights = {}
        for b in range(1, BLOCKS):
            weights = keep.tile([P, S], F32, name="weights%d" % b)
            block_weights[b] = weigh(weights[:], b, cols(0, S))
            for h in range(HALVES):
                half_weights[b, h] = weights[:, cols(h, HALF)]

        def first_stage(b, h, act, sum_a, abs_b):
            acc_a = psum.tile([P, HALF], F32, name="acc_a", tag="bank_a")
            acc_b = psum.tile([P, HALF], F32, name="acc_b", tag="bank_b")
            for a in range(PASSES):
                codes, plane = w1_q[b, a]
                moving = (
                    (acc_a, codes.bitcast(FP8X4), plane),
                    (acc_b, w2_codes[:, a, cols(b, 2 * P)].bitcast(FP4X4), w2_plane[:, a, cols(b, P)]),
                )
                for acc, weight, weight_plane in moving:
                    for g in range(GROUPS):
                        nc.tensor.matmul_mx(
                            out=acc[:, cols(g, P)],
                            lhsT=picked[a][:, cols(h * GROUPS + g, P)].bitcast(FP8X4),
                            lhsT_scale=tab_plane[a][:, cols(h * GROUPS + g, P)],
                            rhs=weight,
                            rhs_scale=weight_plane,
                            start=a == 0 and g == 0,
                            stop=a == LAST_PASS and g == GROUPS - 1,
                        )
            nc.scalar.copy(out=sum_a[:], in_=acc_a[:])
            nc.scalar.activation(out=abs_b[:], in_=acc_b[:], func=ACT.Abs)
            pre = psum.tile([P, HALF], F32, name="pre", tag="bank_c")
            for term, src in enumerate((sum_a, abs_b)):
                for g in range(GROUPS):
                    nc.tensor.matmul(
                        pre[:, cols(g, P)], lhsT=src[:, cols(g, P)], rhs=ident[:], is_transpose=True,
                        start=term == 0 and g == 0, stop=term == 1 and g == GROUPS - 1,
                    )
            nc.scalar.activation(out=act[:, cols(h, HALF)], in_=pre[:], func=ACT.Tanh)

        def scatter(b, offsets, values, weights):
            nc.vector.tensor_tensor(page[b][:].indirect(offsets), values, weights, ALU.mult)

        def scatter_half(b, h, act):
            scatter(b, half_list(idx2, h), act[:, cols(h, HALF)], half_weights[b, h])

        turned = [keep.tile([P, GROUPS, 2, P], F32, name="turned%d" % h) for h in range(HALVES)]

        def turn(b, h, x_rows):
            x_ps = psum.tile([P, HALF], BF16, name="x_ps", tag="bank_d")
            for g in range(GROUPS):
                nc.tensor.transpose(x_ps[:, cols(g, P)], x_rows[:, cols(g, P)], ident_bf[:])
            nc.scalar.copy(
                out=turned[h][:, :, :, cols(b, P // PACK)],
                in_=x_ps[:].bitcast(F32).rearrange("p (g q u) -> p g u q", g=GROUPS, u=2),
            )

        def reread(b, holder):
            got = ring.tile([P, M], F32, name="got")
            x_rows = holder[:].bitcast(BF16)
            nc.vector.tensor_copy(out=got[:], in_=page[b][:].indirect(idx3[:]))
            nc.scalar.activation(out=x_rows, in_=got[:], func=ACT.Copy, scale=row_factor(SC, b))
            for h in range(HALVES):
                turn(b, h, x_rows[:, cols(h, HALF)])

        def reread_last():
            got = ring.tile([P, M], F32, name="got")
            x_half = ring.tile([P, HALF], BF16, name="x_half", bufs=1)
            for h in range(HALVES):
                nc.vector.tensor_copy(out=got[:, cols(h, HALF)], in_=page[LAST_BLOCK][:].indirect(half_list(idx3, h)))
            for h in range(HALVES):
                nc.scalar.activation(
                    out=x_half[:], in_=got[:, cols(h, HALF)], func=ACT.Copy, scale=row_factor(SC, LAST_BLOCK)
                )
                turn(LAST_BLOCK, h, x_half)

        for b in range(BLOCKS):
            if b + 2 < BLOCKS:
                load_w1(b + 2)
            if b + 1 < BLOCKS:
                load_page(b + 1)
            act = ring.tile([P, S], F32, name="act")
            sum_a = ring.tile([P, HALF], F32, name="sum_a", tag="left", bufs=BLOCKS)
            abs_b = ring.tile([P, HALF], F32, name="abs_b", tag="right", bufs=BLOCKS)
            first_stage(b, 0, act, sum_a, abs_b)
            if b < LAST_BLOCK:
                scatter_half(b, 0, act)
            first_stage(b, 1, act, sum_a, abs_b)
            if b == 0:
                half_weights[0, 1] = weigh(prepare_w1(1)[:, K_PASS:].bitcast(F32), 0, cols(1, HALF))
            if b < LAST_BLOCK:
                scatter_half(b, 1, act)
            else:
                scatter(b, idx2[:], act[:], block_weights[b])
            if b + 2 < BLOCKS:
                prepare_w1(b + 2)
            if b > 0:
                reread(b - 1, abs_b)

        w4_raw = keep.tile([P, PACK, H], F32, name="w4_raw")
        nc.sync.dma_start(out=w4_raw[:], in_=w4.rearrange("(p j) c -> p j c", j=PACK))
        w3_codes = keep.tile([P, 2 * H], U8, name="w3_codes", align_bytes=64)
        nc.sync.dma_start(out=w3_codes[:].bitcast(I32), in_=w3_words[0].bitcast(I32))
        for q in range(QUADRANTS):
            nc.sync.dma_start(
                out=w3_plane[quadrant_rows(q), :].bitcast(I32),
                in_=w3_scales[0, cols(q, SCALE_ROWS), :].bitcast(I32),
            )
        w4_grouped = ring.tile([P, H * PACK], BF16, name="w4_grouped", tag="abs_x", align_bytes=64)
        interleave(w4_grouped[:], w4_raw)
        w4_codes, w4_plane = quantise("w4", w4_grouped[:], H)

        nxt = {}

        def gather_next(b, dst):
            nc.vector.tensor_copy(out=dst, in_=page[b][:].indirect(idx4[:]))
            for h in range(HALVES):
                nxt[b, h] = dst[:, cols(h, HALF)]

        def gather_next_half(b, h, dst):
            nc.vector.tensor_copy(out=dst, in_=page[b][:].indirect(half_list(idx4, h)))
            nxt[b, h] = dst

        def turn_back(h):
            x_words = ring.tile([P, HALF, 2], F32, name="x_words", align_bytes=64)
            for pair in range(GROUPS // 2):
                back = psum.tile([P, 2, 2, P], F32, name="back", tag="bank_c")
                for g in range(2):
                    for u in range(2):
                        nc.tensor.transpose(back[:, g, u, :], turned[h][:, 2 * pair + g, u, :], ident[:])
                nc.scalar.copy(
                    out=x_words[:, cols(pair, 2 * P), :].rearrange("p (g m) u -> p g m u", g=2),
                    in_=back[:].rearrange("p g u m -> p g m u"),
                )
            return x_words[:].rearrange("p m u -> p (m u)").bitcast(BF16)

        def quantise_x(h, x_grouped):
            abs_x = ring.tile([P, HALF * PACK], BF16, name="abs_x", tag="abs_x", align_bytes=64)
            for part in range(2):
                span = cols(part, PACK * HALF // 2)
                nc.scalar.activation(out=abs_x[:, span], in_=x_grouped[:, span], func=ACT.Abs)
            return quantise("x%d" % h, x_grouped, HALF), quantise("abs_x%d" % h, abs_x[:], HALF), abs_x

        def finish(b, h, low):
            nc.vector.scalar_tensor_tensor(low[:], low[:], row_factor(GV, b), nxt[b, h], ALU.mult, ALU.mult)
            nc.sync.dma_start(out=out[cols(b, P), cols(h, HALF)], in_=low[:])

        def second_stage(h, x_q, abs_q):
            lows = []
            for b in range(BLOCKS):
                y3 = psum.tile([P, HALF], F32, name="y3", tag="bank_a")
                y4 = psum.tile([P, HALF], F32, name="y4", tag="bank_b")
                nc.tensor.matmul_mx(
                    out=y3[:], lhsT=w3_codes[:, cols(b, 2 * P)].bitcast(FP4X4), lhsT_scale=w3_plane[:, cols(b, P)],
                    rhs=x_q[0][:].bitcast(FP8X4), rhs_scale=x_q[1][:], start=True, stop=True,
                )
                nc.tensor.matmul_mx(
                    out=y4[:], lhsT=w4_codes[:, cols(b, P)].bitcast(FP8X4), lhsT_scale=w4_plane[:, cols(b, P)],
                    rhs=abs_q[0][:].bitcast(FP8X4), rhs_scale=abs_q[1][:], start=True, stop=True,
                )
                y3_sb = ring.tile([P, HALF], F32, name="y3_sb", tag="left", bufs=BLOCKS)
                nc.scalar.copy(out=y3_sb[:], in_=y3[:])
                low = ring.tile([P, HALF], F32, name="low", tag="right", bufs=BLOCKS)
                nc.vector.tensor_tensor(low[:], y4[:], y3_sb[:], ALU.min)
                lows.append(low)
                if b > 0:
                    finish(b - 1, h, lows[b - 1])
            finish(LAST_BLOCK, h, lows[LAST_BLOCK])

        reread_last()
        gather_next_half(0, 0, half_weights[0, 0])
        gather_next(1, act[:])
        gather_next(2, block_weights[3])
        gather_next(3, block_weights[2])
        first_q = quantise_x(0, turn_back(0))[:2]
        x_later = turn_back(1)
        second_stage(0, *first_q)
        later_x_q, later_abs_q, later_abs_x = quantise_x(1, x_later)
        gather_next_half(0, 1, later_abs_x[:, PACK * HALF // 2 :].bitcast(F32))
        second_stage(1, later_x_q, later_abs_q)
